import numpy as np, ml_dtypes
CORES = [242,247,114,119]
N = 4
V, K, ROUNDS = 8192, 4, 3
CAPP = 512
def entries(a): return a.T.reshape(-1)
def pack(v, P): return np.ascontiguousarray(np.asarray(v, np.int32).reshape(-1, P).T)
def lists(rng, how):
    T = V * K; me = np.arange(N)[:, None]
    O = np.broadcast_to(me, (N, T)).copy()
    for r in range(N):
        p = rng.permutation(T); a = 0
        if how == "clump": p = (CAPP * int(rng.integers(T // CAPP)) + np.arange(T)) % T
        if how == "clump" and r % 2: p = 16 * (p % (T // 16)) + p // (T // 16)
        for o in range(N):
            if o != r: c = CAPP if how in ("clump", "full") else int(rng.integers(0, CAPP + 1)); O[r, p[a:a + c]] = o; a += c
    I = V * O + rng.integers(0, V, (N, T))
    if how == "alike": I = V * O + rng.integers(0, V, N)[O]
    if how == "edge": I = V * O + np.where(rng.random((N, T)) < 0.5, 0, V - 1)
    if how == "line": I = np.minimum(V * me + np.arange(T)[None, :] // K + 1, N * V - 1)
    return {"nb": np.stack([pack(i, 16) for i in I])}
def setup_inputs(rng):
    return dict({"x": rng.standard_normal((N, 128, V), dtype=np.float32).astype(ml_dtypes.bfloat16)}, **lists(rng, "uniform"))
def setup_inputs_alike(rng):
    d = setup_inputs(rng); d.update(lists(rng, "alike"))
    for k in ("x",): d[k] = (d[k].astype(np.float32) * 1048576.0).astype(d[k].dtype)
    return d
def setup_inputs_clump(rng):
    d = setup_inputs(rng); d.update(lists(rng, "clump"))
    for k in ("x",): d[k] = (d[k].astype(np.float32) * (1 / 1024.0)).astype(d[k].dtype)
    return d
def setup_inputs_edge(rng):
    d = setup_inputs(rng); d.update(lists(rng, "edge"))
    return d
def setup_inputs_full(rng):
    d = setup_inputs(rng); d.update(lists(rng, "full"))
    return d
def setup_inputs_line(rng):
    d = setup_inputs(rng); d.update(lists(rng, "line"))
    return d
def check_inputs(x):
    bad = []
    if x["nb"].min() < 0 or x["nb"].max() >= N * V: bad.append("nb out of range")
    if np.abs(x["x"].astype(np.float32)).max() > 1e30: bad.append("x beyond -1e30 to 1e30")
    for r in range(N):
        c = np.bincount(entries(x["nb"][r]) // V, minlength=N); c[r] = 0
        if int(c.max()) > CAPP: bad.append("more than CAPP entries of a list point into one other rank's part")
    return bad
def reference(x, nb):
    A = np.concatenate(list(x), axis=1)
    NB = np.concatenate([entries(a) for a in nb]).reshape(N * V, K)
    for k in range(ROUNDS):
        B = A.copy()
        for j in range(K): B = np.maximum(B, A[:, NB[:, j]])
        A = B
    return {"y": np.stack([A[:, V * r:V * r + V] for r in range(N)])}

@@ -1,0 +1,462 @@
+from concourse.bass import DstId, RemoteDMATransfer
+from concourse.mybir import AluOpType, AxisListType, ActivationFunctionType
+
+N = 4
+NCORES = 256
+W = 2432
+TW = 4 * W
+CHUNKS = [(0, 512), (512, 512), (1024, 512), (1536, 256), (1792, 256)]
+OUTCH = [(0, 1024, 1), (1024, 512, 2), (1536, 512, 4)]
+
+SCRATCH = {}
+WHERE = {}
+
+
+def many(names, cols, dtype, where="sbuf", rows=128):
+    for n in names.split():
+        SCRATCH[n] = (where, [rows, cols], dtype)
+        WHERE[n] = (n, 0, cols)
+
+
+def pool(buf, names, cols, dtype):
+    for i, n in enumerate(names.split()):
+        WHERE[n] = (buf, i * cols, cols)
+    SCRATCH[buf] = ("sbuf", [128, cols * len(names.split())], dtype)
+
+
+many("nbt", 256, "int32")
+pool("pi", "t1 orel ui s2 a3 h2 uq", 256, "int32")
+pool("pf", "uf c1 c2 c3 c4 c5 c6 c7 c8 c9 fo cde", 256, "float32")
+many("flg scn", 768, "bfloat16")
+many("zer", 256, "bfloat16")
+many("tot", 4, "bfloat16")
+pool("pmb", "lt idn oneb", 128, "bfloat16")
+pool("pm", "ones zf e0 e1 bq", 128, "float32")
+many("sl w1 w2", 512, "float32")
+many("ab oh", 1536, "float32")
+pool("pc", "ba hf bas tb m4 f1 f2 f3 s0 qp qn", 4, "float32")
+many("gs gm key", 768, "float32")
+many("xb", 3072, "float32")
+many("rq0 rqs rq", 12, "float32")
+pool("pci", "ip iq i15 i16 i4", 1, "int32")
+many("offm", 512, "uint16")
+pool("pvi", "vi vs v4 v3", 24, "int32")
+pool("pvf", "vc vt vw vz", 24, "float32")
+pool("pvo", "offu o4 o3", 24, "uint16")
+many("full", 2048, "float32")
+many("cd", 2048, "float32", "dram", 16)
+many("xg mg xm", 384, "float32")
+pool("pz", "z0 z1 z2 z3 z4 z5 z6 z7 z8", 96, "float32")
+many("offn", 96, "uint16")
+many("tab0 tab1 tab2", TW, "bfloat16")
+many("res mk0 mk st1 st2 st3 ot1 ot2 ot3", 2048, "bfloat16")
+many("h0 h1 h2v lh0", 384, "bfloat16")
+many("gat sca", 9728, "bfloat16")
+many("own", 2048, "float32", "psum")
+many("k0 k1 k2 msc", 512, "float32", "psum")
+SEMAPHORES = (["sv", "ss", "sp", "sg", "ex", "cw", "cr", "nbl", "xl0", "ld1", "ld2", "ld3", "nba", "xa", "rqa",
+               "ha0", "ha1", "ha2", "ls", "yd"] + ["oa%d_%d" % (b, c) for b in (1, 2, 3) for c in range(len(OUTCH))])
+
+
+def rank_program(g, core, T, topo):
+    team = {}
+    for r in range(N):
+        rc = T.cores[r]
+        team[r] = [rc] + [c for c in range(NCORES) if c != rc and topo.host(c) == topo.host(rc)
+                          and topo.chip(c) == topo.chip(rc) and topo.die(c) == topo.die(rc)]
+    r = b = None
+    for rr in range(N):
+        if core in team[rr]:
+            r, b = rr, team[rr].index(core)
+    if r is None:
+        return
+    A, F = AluOpType, ActivationFunctionType
+    v, sc, pe, sy = g.vector, g.scalar, g.tensor, g.sync
+    Q = {"v": v, "s": sc, "p": pe, "y": sy, "g": g}
+    cnt, seen = {"v": 0, "s": 0, "p": 0, "g": 0}, {}
+
+    def X(name, a=0, e=None, step=1, lo=0, hi=128):
+        buf, c0, n = WHERE[name]
+        e = n if e is None else e
+        if step == 1:
+            return T[buf][lo:hi, c0 + a:c0 + e]
+        return T[buf][lo:hi, c0 + a:c0 + e:step]
+
+    def col(name, k=0):
+        return X(name, k, k + 1)
+
+    def need(q, *tickets):
+        for t in tickets:
+            sem, n = t
+            if seen.get((q, sem), 0) < n:
+                Q[q].wait_ge(T.sem[sem], n)
+                seen[(q, sem)] = n
+
+    def done(q, ins):
+        ins.then_inc(T.sem["s" + q], 1)
+        cnt[q] += 1
+        return ("s" + q, cnt[q])
+
+    dcnt = {}
+
+    def dma(q, sem, out, in_):
+        Q[q].dma_start(out, in_).then_inc(T.sem[sem], 16)
+        dcnt[sem] = dcnt.get(sem, 0) + 16
+        return (sem, dcnt[sem])
+
+    def ts(out, a, s1, op0, s2=None, op1=None, w=()):
+        need("v", *w)
+        if op1 is None:
+            return done("v", v.tensor_scalar(out, a, s1, None, op0))
+        return done("v", v.tensor_scalar(out, a, s1, s2, op0, op1))
+
+    def tt(out, a, c, op, w=()):
+        need("v", *w)
+        return done("v", v.tensor_tensor(out, a, c, op))
+
+    def cp(out, a, w=()):
+        need("v", *w)
+        return done("v", v.tensor_copy(out, a))
+
+    def fill(ap, c):
+        return done("v", v.memset(ap, c))
+
+    def mm(out, l, rh, w=()):
+        need("p", *w)
+        return done("p", pe.matmul(out, l, rh, True, True))
+
+    def bits(m):
+        return [1 << i for i in range(16) if m >> i & 1]
+    oth = [(r + 1 + k) % N for k in range(3)]
+    peer = [team[o][b] for o in oth]
+    my = [(r - o - 1) % N for o in oth]
+    off = [p for p in peer if (topo.host(p), topo.chip(p)) != (topo.host(core), topo.chip(core))]
+    offbits = bits(topo.mask(core, off[0]))
+    half = len(offbits) // 2
+    masks = []
+    for p in peer:
+        if p in off:
+            k = off.index(p)
+            masks.append(sum(offbits[k * half:(k + 1) * half]))
+        else:
+            masks.append(sum(x for x in bits(topo.mask(core, p)) if x not in offbits))
+    NIN = sum(bin(m).count("1") for m in masks)
+    lsn = [0]
+
+    def did(p):
+        rid, pid = topo.addr(p, core)
+        return DstId(rid=rid, pnc=pid)
+
+    def fused3(srcs, dsts, sem):
+        tr = [RemoteDMATransfer(dst_ids=[did(p)], dma_engine_mask=masks[k], remote_sem=T.sem[sem],
+                                srcs=[srcs[k]], dsts=[dsts[k]]) for k, p in enumerate(peer)]
+        g.remote_dma_fused(tr, local_sem=T.sem["ls"])
+        lsn[0] += NIN
+
+    def rotate(q, sem, t, c0, n, src=None, w=()):
+        need(q, *w)
+        last = None
+        for d in (1, 2, 3):
+            s, k = (t, c0) if src is None else (src, 0)
+            cut = 128 - 32 * d
+            last = dma(q, sem, t[0:cut, W * d + c0:W * d + c0 + n], s[32 * d:128, k:k + n])
+            last = dma(q, sem, t[cut:128, W * d + c0:W * d + c0 + n], s[0:32 * d, k:k + n])
+        return last
+
+    tabs = [T.tab0, T.tab1, T.tab2]
+    stage = [None, T.st1, T.st2, T.st3]
+
+    xl = None
+    if b == 0:
+        for ch in range(8):
+            nbw = dma("ys"[ch % 2], "nbl", T.nbt[16 * ch:16 * ch + 16, :], T.nb[:, 256 * ch:256 * ch + 256])
+        for k in (1, 2, 3):
+            for q in range(4):
+                dma("ys"[q % 2], "ld%d" % k, stage[k][32 * q:32 * q + 32, :], T.x[32 * k:32 * k + 32, 2048 * q:2048 * q + 2048])
+        for d in range(4):
+            for q in range(4):
+                s = 2048 * ((q + d) % 4)
+                xl = dma("ys"[q % 2], "xl0", T.tab0[32 * q:32 * q + 32, W * d:W * d + 2048], T.x[0:32, s:s + 2048])
+    else:
+        nbw = ("nba", 16)
+
+    vo = fill(X("ones"), 1.0)
+    vob = fill(X("oneb"), 1.0)
+    vzf = fill(X("zf"), 0.0)
+    vz = fill(X("zer"), 0.0)
+
+    def sel(out, in_, pat, op, fl, base, cm, w=()):
+        need("g", *w)
+        return done("g", g.affine_select(out, in_, pat, op, fl, base, cm))
+
+    gip = done("g", g.iota(X("ip"), [[0, 1]], 0, 1))
+    gsl = None
+    for k in range(4):
+        gsl = done("g", g.iota(X("sl", 128 * k, 128 * k + 128), [[1, 4], [256, 2], [4, 16]], 64 * k, 0,
+                               allow_small_or_imprecise_dtypes=True))
+    x1 = sel(X("lt"), X("oneb"), [[1, 128]], A.is_gt, 0.0, 0, -1, (vob,))
+    glt = sel(X("lt"), X("lt"), [[1, 128]], A.not_equal, 0.5, 0, -1, (x1,))
+    if b == 0:
+        need("g", nbw)
+        m = topo.mask(core, team[r][1])
+        g.remote_dma_fused([RemoteDMATransfer(dst_ids=[did(p) for p in team[r][1:]], dma_engine_mask=m,
+                                              remote_sem=T.sem["nba"], srcs=[T.nbt[:]], dsts=[T.nbt[:]] * 3)],
+                           local_sem=T.sem["ls"])
+        lsn[0] += bin(m).count("1")
+    ge = [sel(X(e), X("ones"), [[-32, 4], [0, 2], [-1, 16]], A.is_equal, 0.0, -16 * k, 1, (vo,))
+          for k, e in enumerate(("e0", "e1"))]
+    gid = sel(X("idn"), X("oneb"), [[1, 128]], A.is_equal, 0.0, 0, -1)
+    if b == 0:
+        for k in (1, 2, 3):
+            p = team[r][k]
+            m = topo.mask(core, p)
+            rid, pid = topo.addr(p, core)
+            need("g", ("ld%d" % k, 64))
+            g.remote_dma(T.tab0[:, 0:2048], stage[k][:], T.sem["xa"], T.sem["ls"], pid, rid, m)
+            lsn[0] += bin(m).count("1")
+    gbq = None
+    for k in range(4):
+        gbq = sel(X("bq"), X("zf") if k == 0 else X("bq"), [[-16, 8], [0, 4], [-1, 4]], A.not_equal, 1.0, -4 * k, 1,
+                  (vzf,) if k == 0 else (gbq,))
+
+    a1 = ts(X("iq"), X("ip"), 5, A.logical_shift_right, w=(gip,))
+    a2 = ts(X("i15"), X("ip"), 15, A.bitwise_and)
+    a3 = ts(X("i16"), X("ip"), 16, A.bitwise_and)
+    a4 = ts(X("i4"), X("ip"), 2, A.logical_shift_right, 3, A.bitwise_and)
+    a5 = ts(col("qp"), X("iq"), float(W), A.mult, w=(a1,))
+    vq = ts(col("qn"), X("iq"), float(-W), A.mult)
+    a6 = ts(col("f1"), X("i15"), 4.0, A.mult, w=(a2,))
+    a7 = ts(col("f2"), X("i16"), 16.0, A.mult, w=(a3,))
+    vm4 = None
+    for k in range(4):
+        vm4 = ts(col("m4", k), X("i4"), float(k), A.is_equal, w=(a4,))
+    a8 = tt(col("f3"), col("f1"), col("f2"), A.add, (a6, a7))
+    a9 = tt(col("s0"), col("f3"), X("iq"), A.add, (a8,))
+    vtb = None
+    for k in range(4):
+        vtb = ts(col("tb", k), col("s0"), -16384.0, A.mult, -16384.0 * (64 * k + 1), A.add, (a9,))
+    need("v", fill(X("mk0"), 9e29))
+    a1 = fill(X("mk0", 0, 2048, 4), -9e29)
+    vmk = ts(X("mk"), X("mk0"), 4.0, A.mult, w=(a1,))
+    vh = None
+    for d in range(4):
+        vh = fill(T.tab0[:, W * d + 2048:W * d + W], 0.0)
+
+    a1 = ts(X("t1"), X("nbt"), float(8192 * (3 - r)), A.add, w=(nbw,))
+    vu = ts(X("ui"), X("nbt"), 8191, A.bitwise_and)
+    vor = ts(X("orel"), X("t1"), 13, A.logical_shift_right, 3, A.bitwise_and, (a1,))
+    vuf = cp(X("uf"), X("ui"), (vu,))
+    fl, ns = [], []
+    for k in range(3):
+        fl.append(ts(X("flg", 256 * k, 256 * k + 256), X("orel"), float(k), A.is_equal, w=(vor,)))
+    for k in range(3):
+        need("v", fl[k], vz)
+        ns.append(done("v", v.tensor_tensor_scan(X("scn", 256 * k, 256 * k + 256), X("zer"), X("flg", 256 * k, 256 * k + 256),
+                                                 0.0, A.add, A.add)))
+    vt = cp(X("tot", 0, 3), X("scn", 255, 768, 256), (ns[2],))
+    pb = mm(X("msc", 0, 3), X("lt"), X("tot", 0, 3), (vt, glt))
+    vhf = ts(X("hf", 0, 3), X("tot", 0, 3), 0.5, A.mult, w=(vt,))
+    vba = ts(X("ba", 0, 3), X("msc", 0, 3), -1.0, A.mult, 0.5, A.add, (pb,))
+    vbs = tt(X("bas", 0, 3), X("msc", 0, 3), X("hf", 0, 3), A.subtract, (pb, vhf))
+    sab = []
+    need("s", vba, gsl)
+    for k in range(3):
+        sab.append(done("s", sc.activation(X("ab", 512 * k, 512 * k + 512), X("sl"), F.Abs, bias=col("ba", k))))
+    kb = ["k0", "k1", "k2"]
+    sx, vg, jobs = [], [], []
+
+    tk = {}
+    jobs.append(lambda: tk.update(a=ts(X("uq"), X("ui"), 11, A.logical_shift_right)))
+    jobs.append(lambda: tk.update(fo=ts(X("fo"), X("orel"), 3.0, A.is_equal)))
+    jobs.append(lambda: tk.update(b=ts(X("c5"), X("uq"), 384.0, A.mult, -9727.0, A.add, (tk["a"],))))
+    jobs.append(lambda: tk.update(o=ts(X("c3"), X("orel"), 512.0, A.mult, -1.0, A.add)))
+    jobs.append(lambda: tk.update(c=tt(X("c6"), X("c5"), X("uf"), A.add, (tk["b"],))))
+    jobs.append(lambda: tk.update(d=tt(X("c1"), X("gm", 0, 256), X("gm", 256, 512), A.add, (vg[1],))))
+    jobs.append(lambda: tk.update(e=tt(X("c7"), X("c6"), X("fo"), A.mult, (tk["c"], tk["fo"]))))
+    jobs.append(lambda: tk.update(f=tt(X("c2"), X("c1"), X("gm", 512, 768), A.add, (tk["d"], vg[2]))))
+    jobs.append(lambda: tk.update(g=ts(X("c4"), X("c2"), 1.0 / 16384.0, A.mult, w=(tk["f"],))))
+    jobs.append(lambda: tk.update(h=tt(X("s2"), X("c4"), X("c3"), A.add, (tk["g"], tk["o"]))))
+    jobs.append(lambda: tk.update(i=ts(X("a3"), X("s2"), 3, A.bitwise_and, w=(tk["h"],))))
+    jobs.append(lambda: tk.update(j=ts(X("h2"), X("s2"), 2, A.logical_shift_right)))
+    jobs.append(lambda: tk.update(k=ts(X("c8"), X("a3"), float(W), A.mult, 2048.0, A.add, (tk["i"],))))
+    jobs.append(lambda: tk.update(l=tt(X("c9"), X("c8"), X("h2"), A.add, (tk["k"], tk["j"]))))
+    jobs.append(lambda: tk.update(z=tt(X("cde"), X("c9"), X("c7"), A.add, (tk["l"], tk["e"]))))
+
+    vr = []
+
+    def reduces(k):
+        for m in range(4):
+            i = 4 * k + m
+            need("v", sx[i])
+            vr.append(done("v", v.tensor_reduce(col("rq0", i), X("xb", 256 * i, 256 * i + 256), AxisListType.X, A.min,
+                                                apply_absolute_value=True)))
+            if k * 4 + m < 5:
+                jobs.pop(0)()
+
+    for k in range(3):
+        c, e = 256 * k, 256 * k + 256
+        x1 = ts(X("gs", c, e), X("scn", c, e), col("bas", k), A.add, 16384.0, A.mult, (vbs,))
+        voh = ts(X("oh", 512 * k, 512 * k + 512), X("ab", 512 * k, 512 * k + 512), col("hf", k), A.is_lt, w=(sab[k], vhf))
+        vg.append(tt(X("gm", c, e), X("gs", c, e), X("flg", c, e), A.mult, (x1,)))
+        vk = tt(X("key", c, e), X("gm", c, e), X("uf"), A.add, (vg[k], vuf))
+        for m in range(4):
+            i = 4 * k + m
+            ps = kb[i % 3]
+            p1 = mm(X(ps, 0, 256), X("oh", 512 * k + 128 * m, 512 * k + 128 * m + 128), X("key", c, e),
+                    (vk, voh) + ((sx[i - 3],) if i >= 3 else ()))
+            need("s", p1, vtb)
+            sx.append(done("s", sc.activation(X("xb", 256 * i, 256 * i + 256), X(ps, 0, 256), F.Identity, bias=col("tb", m))))
+        if k:
+            reduces(k - 1)
+    reduces(2)
+    vrq = ts(X("rqs"), X("rq0"), 8191.0, A.min, w=(vr[-1],))
+    need("g", vrq)
+    fused3([X("rqs", 4 * k, 4 * k + 4) for k in range(3)], [X("rq", 4 * my[k], 4 * my[k] + 4) for k in range(3)], "rqa")
+    while jobs:
+        jobs.pop(0)()
+    vcd = tk["z"]
+    need("s", vcd)
+    for ch in range(8):
+        cw = dma("s", "cw", T.cd[:, 256 * ch:256 * ch + 256], X("cde", lo=16 * ch, hi=16 * ch + 16))
+    need("s", cw)
+    for k in range(8):
+        cr = dma("s", "cr", T.full[16 * k:16 * k + 16, :], T.cd[:, :])
+    mm(X("k0", 0, 256), X("e0"), X("cde"), (vcd, ge[1], sx[9]))
+    pc = mm(X("k0", 256, 512), X("e1"), X("cde"))
+
+    if b == 0:
+        xw = xl
+    else:
+        xw = rotate("y", "ex", T.tab0, 0, 2048, w=(("xa", 16),))
+    xown = xl if b == 0 else ("xa", 16)
+    po = []
+    for m in range(4):
+        po.append(mm(X("own", 512 * m, 512 * m + 512), X("idn"), T.tab0[:, 512 * m:512 * m + 512], (xown, gid)))
+
+    x1 = ts(X("w1"), X("k0"), col("qp"), A.is_lt, float(TW), A.mult, (pc,))
+    x2 = tt(X("w2"), X("w1"), X("k0"), A.add, (x1,))
+    voff = ts(X("offm"), X("w2"), col("qn"), A.add, w=(x2,))
+
+    pu = None
+    for k in range(3):
+        for h in range(2):
+            pu = mm(X("msc", 8 * k + 4 * h, 8 * k + 4 * h + 4), X(("e0", "e1")[h]), X("rq", 4 * k, 4 * k + 4),
+                    (("rqa", NIN), vbs, vba))
+    x0 = cp(X("vi"), X("msc", 0, 24), (pu,))
+    x1 = ts(X("vs"), X("vi"), 11, A.logical_shift_right, w=(x0,))
+    u4 = ts(X("v4"), X("vi"), 2, A.logical_shift_right)
+    x2 = ts(X("vc"), X("vs"), 384.0, A.mult, w=(x1,))
+    u3 = ts(X("v3"), X("vi"), 3, A.bitwise_and)
+    x3 = tt(X("vt"), X("vc"), X("vi"), A.add, (x2,))
+    o4 = cp(X("o4"), X("v4"), (u4,))
+    x4 = ts(X("vw"), X("vt"), col("qp"), A.is_lt, float(TW), A.mult, (x3,))
+    o3 = cp(X("o3"), X("v3"), (u3,))
+    x5 = tt(X("vz"), X("vt"), X("vw"), A.add, (x4,))
+    vou = ts(X("offu"), X("vz"), col("qn"), A.add, w=(x5,))
+    need("v", xown, xw, vh, vou)
+    vh0 = cp(T.h0[:], T.tab0[:, 0:TW].indirect(X("offu")))
+    need("g", vh0)
+
+    def hsend(src, dst, c0, sem):
+        fused3([src[:, 128 * k:128 * k + 128] for k in range(3)],
+               [dst[:, c0 + 128 * my[k]:c0 + 128 * my[k] + 128] for k in range(3)], sem)
+    hsend(T.h0, T.lh0, 0, "ha0")
+    need("v", o4, cr)
+    y1 = cp(X("xg"), T.full[:, 0:2048].indirect(X("o4")))
+    need("v", o3, vm4)
+    y2 = cp(X("mg"), X("m4").indirect(X("o3")))
+    y3 = tt(X("xm"), X("xg"), X("mg"), A.mult, (y1, y2))
+    pz = mm(X("k1", 0, 384), X("bq"), X("xm"), (y3, gbq, sx[10]))
+    zt = [ts(X("z%d" % k), X("k1", k, 384, 4), col("m4", k), A.mult, w=(pz,)) for k in range(4)]
+    y4 = tt(X("z4"), X("z0"), X("z1"), A.add, (zt[1],))
+    y5 = tt(X("z5"), X("z2"), X("z3"), A.add, (zt[3],))
+    y6 = tt(X("z6"), X("z4"), X("z5"), A.add, (y4, y5))
+    y7 = ts(X("z7"), X("z6"), col("qp"), A.is_lt, float(TW), A.mult, (y6,))
+    y8 = tt(X("z8"), X("z6"), X("z7"), A.add, (y7,))
+    von = ts(X("offn"), X("z8"), col("qn"), A.add, w=(y8,))
+    need("y", ("ha0", NIN), vh0, xw)
+    dma("y", "ex", T.tab0[:, 2048:W], T.lh0[:])
+    ready = [rotate("y", "ex", T.tab0, 2048, 384, T.lh0), xw, xown]
+
+    hv = [None, T.h1, T.h2v]
+    lastv = von
+    for s in range(3):
+        tin = tabs[s]
+        tout = tabs[s + 1] if s < 2 else T.res
+        units = []
+        if s < 2:
+            units.append((None, 0, 384, 0, "offn", 0))
+        for c, (c0, n) in enumerate(CHUNKS):
+            units.append((c, c0, n, 1536 + 4 * c0, "offm", c0 // 4))
+        need("s", von, voff, lastv, *ready)
+        need("v", von, voff, vmk, *ready)
+        sg, vgs = [], []
+        for (c, c0, n, g0, of, k0) in units:
+            e = 3 * n
+            sg.append(done("s", sc.activation(T.gat[:, g0:g0 + e], tin[:, 0:TW].indirect(X(of, k0, k0 + e // 16)), F.Copy)))
+
+        def vgather(i):
+            c, c0, n, g0, of, k0 = units[i]
+            e = 3 * n
+            vgs.append(cp(T.gat[:, g0 + e:g0 + 4 * n], tin[:, 0:TW].indirect(X(of, k0 + e // 16, k0 + n // 4))))
+
+        vgather(0)
+        nready = []
+        for i, (c, c0, n, g0, of, k0) in enumerate(units):
+            if i + 1 < len(units):
+                vgather(i + 1)
+            need("v", sg[i], vgs[i])
+            x1 = done("v", v.tensor_tensor_scan(T.sca[:, g0:g0 + 4 * n], T.mk[:, 0:4 * n], T.gat[:, g0:g0 + 4 * n], 0.0,
+                                                A.min, A.max))
+            if c is None:
+                need("v", x1)
+                x2 = done("v", v.tensor_tensor(hv[s + 1][:], tin[:, 0:TW].indirect(X("offu")),
+                                               T.sca[:, g0 + 3:g0 + 4 * n:4], A.max))
+                need("g", x2)
+                hsend(hv[s + 1], tout, 2048, "ha%d" % (s + 1))
+                continue
+            lastv = tt(tout[:, c0:c0 + n], T.sca[:, g0 + 3:g0 + 4 * n:4], T.own[:, c0:c0 + n], A.max, (x1, po[c0 // 512]))
+            if s < 2:
+                nready = [rotate("y", "ex", tout, c0, n, w=(lastv,))]
+                if c == 2:
+                    nready = [rotate("y", "ex", tout, 2048, 384, w=(("ha%d" % (s + 1), NIN),))]
+                if (c0 + n) % 512 == 0:
+                    m = c0 // 512
+                    po[m] = mm(T.own[:, 512 * m:512 * m + 512], X("idn"), tout[:, 512 * m:512 * m + 512], (lastv,))
+            else:
+                for j, (o0, on, oc) in enumerate(OUTCH):
+                    if oc != c:
+                        continue
+                    if b:
+                        p = team[r][0]
+                        m = topo.mask(core, p)
+                        rid, pid = topo.addr(p, core)
+                        need("g", lastv)
+                        g.remote_dma((None, T.ot1, T.ot2, T.ot3)[b][:, o0:o0 + on], T.res[:, o0:o0 + on],
+                                     T.sem["oa%d_%d" % (b, j)], T.sem["ls"], pid, rid, m)
+                        lsn[0] += bin(m).count("1")
+                    else:
+                        lastj = j == len(OUTCH) - 1
+                        for k in range(4):
+                            q = "s" if lastj and k % 2 else "y"
+                            if k:
+                                m = topo.mask(team[r][k], core)
+                                need(q, ("oa%d_%d" % (k, j), bin(m).count("1")))
+                            else:
+                                need(q, lastv)
+                            src = (T.res, T.ot1, T.ot2, T.ot3)[k]
+                            for h in range(4):
+                                yd = dma(q, "yd", T.y[32 * k:32 * k + 32, 2048 * h + o0:2048 * h + o0 + on],
+                                         src[32 * h:32 * h + 32, o0:o0 + on])
+        if s < 2:
+            ready = nready + [("ha%d" % (s + 1), NIN), lastv]
+    if b == 0:
+        need("y", yd)
+    need("g", ("ls", lsn[0]))
+    for q in "vspg":
+        need("y", ("s" + q, cnt[q]))
+    if b == 0:
+        need("y", xl)
+    else:
+        need("y", ("nba", 16), ("xa", 16))
+    need("y", ("cr", dcnt["cr"]), ("cw", dcnt["cw"]), ("ex", dcnt["ex"]))

@@ -5,8 +5,8 @@ N = 4
 NCORES = 256
 W = 2432
 TW = 4 * W
-CHUNKS = [(0, 512), (512, 512), (1024, 512), (1536, 256), (1792, 256)]
-OUTCH = [(0, 1024, 1), (1024, 512, 2), (1536, 512, 4)]
+CHUNKS = [(0, 512), (512, 512), (1024, 384), (1408, 384), (1792, 256)]
+OUTCH = [(0, 1024, 1), (1024, 384, 2), (1408, 384, 3), (1792, 256, 4)]
 
 SCRATCH = {}
 WHERE = {}
@@ -25,23 +25,26 @@ def pool(buf, names, cols, dtype):
 
 
 many("nbt", 256, "int32")
-pool("pi", "t1 orel ui s2 a3 h2 uq", 256, "int32")
-pool("pf", "uf c1 c2 c3 c4 c5 c6 c7 c8 c9 fo cde", 256, "float32")
+pool("pi", "t1 orel ui s2 a3 h2 uq t2 uh ul", 256, "int32")
+pool("pf", "uf c2 c4 c9 fo cde", 256, "float32")
 many("flg scn", 768, "bfloat16")
 many("zer", 256, "bfloat16")
 many("tot", 4, "bfloat16")
-pool("pmb", "lt idn oneb", 128, "bfloat16")
+pool("pmb", "lt idn oneb rot1 rot2 rot3", 128, "bfloat16")
 pool("pm", "ones zf e0 e1 bq", 128, "float32")
 many("sl w1 w2", 512, "float32")
-many("ab oh", 1536, "float32")
-pool("pc", "ba hf bas tb m4 f1 f2 f3 s0 qp qn", 4, "float32")
-many("gs gm key", 768, "float32")
+many("ab", 1536, "float32")
+many("oh", 1536, "float16")
+many("ka", 768, "float16")
+many("kl", 256, "float16")
+pool("pc", "ba hf bas b64 tb m4 f1 f2 f3 s0 qp qn q2", 4, "float32")
+many("gm", 768, "float32")
 many("xb", 3072, "float32")
 many("rq0 rqs rq", 12, "float32")
 pool("pci", "ip iq i15 i16 i4", 1, "int32")
 many("offm", 512, "uint16")
 pool("pvi", "vi vs v4 v3", 24, "int32")
-pool("pvf", "vc vt vw vz", 24, "float32")
+pool("pvf", "vc vt vw vz vy", 24, "float32")
 pool("pvo", "offu o4 o3", 24, "uint16")
 many("full", 2048, "float32")
 many("cd", 2048, "float32", "dram", 16)
@@ -54,7 +57,9 @@ many("h0 h1 h2v lh0", 384, "bfloat16")
 many("gat sca", 9728, "bfloat16")
 many("own", 2048, "float32", "psum")
 many("k0 k1 k2 msc", 512, "float32", "psum")
-SEMAPHORES = (["sv", "ss", "sp", "sg", "ex", "cw", "cr", "nbl", "xl0", "ld1", "ld2", "ld3", "nba", "xa", "rqa",
+for _i, _n in enumerate("gs0 p0 gs1 p1 gs2 p2 uh16 p3".split()):
+    WHERE[_n] = ("own", 256 * _i, 256)
+SEMAPHORES = (["sv", "ss", "sp", "sg", "ex", "cw", "cr", "nbl", "xl0", "ld1", "ld2", "ld3", "nba", "xa", "rqa", "gi1", "gi2",
                "ha0", "ha1", "ha2", "ls", "yd"] + ["oa%d_%d" % (b, c) for b in (1, 2, 3) for c in range(len(OUTCH))])
 
 
@@ -118,12 +123,16 @@ def rank_program(g, core, T, topo):
         need("v", *w)
         return done("v", v.tensor_copy(out, a))
 
+    def ac(out, a, w=()):
+        need("s", *w)
+        return done("s", sc.activation(out, a, F.Copy))
+
     def fill(ap, c):
         return done("v", v.memset(ap, c))
 
-    def mm(out, l, rh, w=()):
+    def mm(out, l, rh, w=(), start=True, stop=True):
         need("p", *w)
-        return done("p", pe.matmul(out, l, rh, True, True))
+        return done("p", pe.matmul(out, l, rh, start, stop))
 
     def bits(m):
         return [1 << i for i in range(16) if m >> i & 1]
@@ -153,14 +162,13 @@ def rank_program(g, core, T, topo):
         g.remote_dma_fused(tr, local_sem=T.sem["ls"])
         lsn[0] += NIN
 
-    def rotate(q, sem, t, c0, n, src=None, w=()):
+    def rotate(q, sem, t, c0, n, w=()):
         need(q, *w)
         last = None
         for d in (1, 2, 3):
-            s, k = (t, c0) if src is None else (src, 0)
             cut = 128 - 32 * d
-            last = dma(q, sem, t[0:cut, W * d + c0:W * d + c0 + n], s[32 * d:128, k:k + n])
-            last = dma(q, sem, t[cut:128, W * d + c0:W * d + c0 + n], s[0:32 * d, k:k + n])
+            last = dma(q, sem, t[0:cut, W * d + c0:W * d + c0 + n], t[32 * d:128, c0:c0 + n])
+            last = dma(q, sem, t[cut:128, W * d + c0:W * d + c0 + n], t[0:32 * d, c0:c0 + n])
         return last
 
     tabs = [T.tab0, T.tab1, T.tab2]
@@ -168,20 +176,26 @@ def rank_program(g, core, T, topo):
 
     xl = None
     if b == 0:
-        for ch in range(8):
-            nbw = dma("ys"[ch % 2], "nbl", T.nbt[16 * ch:16 * ch + 16, :], T.nb[:, 256 * ch:256 * ch + 256])
-        for k in (1, 2, 3):
+        def xload(k):
             for q in range(4):
                 dma("ys"[q % 2], "ld%d" % k, stage[k][32 * q:32 * q + 32, :], T.x[32 * k:32 * k + 32, 2048 * q:2048 * q + 2048])
+        for ch in range(8):
+            nbw = dma("ys"[ch % 2], "nbl", T.nbt[16 * ch:16 * ch + 16, :], T.nb[:, 256 * ch:256 * ch + 256])
+        xload(1)
+        need("y", ("gi1", 1))
+        need("s", ("gi1", 1))
+        xload(2)
+        xload(3)
+        need("y", ("gi2", 1))
         for d in range(4):
             for q in range(4):
                 s = 2048 * ((q + d) % 4)
-                xl = dma("ys"[q % 2], "xl0", T.tab0[32 * q:32 * q + 32, W * d:W * d + 2048], T.x[0:32, s:s + 2048])
+                xl = dma("y", "xl0", T.tab0[32 * q:32 * q + 32, W * d:W * d + 2048], T.x[0:32, s:s + 2048])
     else:
         nbw = ("nba", 16)
 
-    vo = fill(X("ones"), 1.0)
     vob = fill(X("oneb"), 1.0)
+    vo = fill(X("ones"), 1.0)
     vzf = fill(X("zf"), 0.0)
     vz = fill(X("zer"), 0.0)
 
@@ -189,11 +203,15 @@ def rank_program(g, core, T, topo):
         need("g", *w)
         return done("g", g.affine_select(out, in_, pat, op, fl, base, cm))
 
+    def xsend(k):
+        p = team[r][k]
+        m = topo.mask(core, p)
+        rid, pid = topo.addr(p, core)
+        need("g", ("ld%d" % k, 64))
+        g.remote_dma(T.tab0[:, 0:2048], stage[k][:], T.sem["xa"], T.sem["ls"], pid, rid, m)
+        lsn[0] += bin(m).count("1")
+
     gip = done("g", g.iota(X("ip"), [[0, 1]], 0, 1))
-    gsl = None
-    for k in range(4):
-        gsl = done("g", g.iota(X("sl", 128 * k, 128 * k + 128), [[1, 4], [256, 2], [4, 16]], 64 * k, 0,
-                               allow_small_or_imprecise_dtypes=True))
     x1 = sel(X("lt"), X("oneb"), [[1, 128]], A.is_gt, 0.0, 0, -1, (vob,))
     glt = sel(X("lt"), X("lt"), [[1, 128]], A.not_equal, 0.5, 0, -1, (x1,))
     if b == 0:
@@ -203,28 +221,34 @@ def rank_program(g, core, T, topo):
                                               remote_sem=T.sem["nba"], srcs=[T.nbt[:]], dsts=[T.nbt[:]] * 3)],
                            local_sem=T.sem["ls"])
         lsn[0] += bin(m).count("1")
+        g.sem_inc(T.sem["gi1"], 1)
+    gsl = None
+    for k in range(4):
+        gsl = done("g", g.iota(X("sl", 128 * k, 128 * k + 128), [[1, 4], [256, 2], [4, 16]], 64 * k, 0,
+                               allow_small_or_imprecise_dtypes=True))
     ge = [sel(X(e), X("ones"), [[-32, 4], [0, 2], [-1, 16]], A.is_equal, 0.0, -16 * k, 1, (vo,))
           for k, e in enumerate(("e0", "e1"))]
-    gid = sel(X("idn"), X("oneb"), [[1, 128]], A.is_equal, 0.0, 0, -1)
     if b == 0:
-        for k in (1, 2, 3):
-            p = team[r][k]
-            m = topo.mask(core, p)
-            rid, pid = topo.addr(p, core)
-            need("g", ("ld%d" % k, 64))
-            g.remote_dma(T.tab0[:, 0:2048], stage[k][:], T.sem["xa"], T.sem["ls"], pid, rid, m)
-            lsn[0] += bin(m).count("1")
+        xsend(1)
+    gid = sel(X("idn"), X("oneb"), [[1, 128]], A.is_equal, 0.0, 0, -1)
     gbq = None
     for k in range(4):
         gbq = sel(X("bq"), X("zf") if k == 0 else X("bq"), [[-16, 8], [0, 4], [-1, 4]], A.not_equal, 1.0, -4 * k, 1,
                   (vzf,) if k == 0 else (gbq,))
+    if b == 0:
+        xsend(2)
+        xsend(3)
+        g.sem_inc(T.sem["gi2"], 1)
+    gro = [sel(X("rot%d" % d), X("zer", 0, 128), [[-1, 128]], A.not_equal, 1.0, -32 * d, 1, (vz,)) for d in (1, 2, 3)]
+    gro = [sel(X("rot%d" % d), X("rot%d" % d), [[-1, 128]], A.not_equal, 1.0, 128 - 32 * d, 1, (gro[d - 1],)) for d in (1, 2, 3)]
 
     a1 = ts(X("iq"), X("ip"), 5, A.logical_shift_right, w=(gip,))
     a2 = ts(X("i15"), X("ip"), 15, A.bitwise_and)
     a3 = ts(X("i16"), X("ip"), 16, A.bitwise_and)
     a4 = ts(X("i4"), X("ip"), 2, A.logical_shift_right, 3, A.bitwise_and)
     a5 = ts(col("qp"), X("iq"), float(W), A.mult, w=(a1,))
-    vq = ts(col("qn"), X("iq"), float(-W), A.mult)
+    a5 = ts(col("qn"), X("iq"), float(-W), A.mult)
+    vq = ts(col("q2"), X("iq"), 2048.0, A.mult)
     a6 = ts(col("f1"), X("i15"), 4.0, A.mult, w=(a2,))
     a7 = ts(col("f2"), X("i16"), 16.0, A.mult, w=(a3,))
     vm4 = None
@@ -234,18 +258,16 @@ def rank_program(g, core, T, topo):
     a9 = tt(col("s0"), col("f3"), X("iq"), A.add, (a8,))
     vtb = None
     for k in range(4):
-        vtb = ts(col("tb", k), col("s0"), -16384.0, A.mult, -16384.0 * (64 * k + 1), A.add, (a9,))
+        vtb = ts(col("tb", k), col("s0"), -16384.0, A.mult, -16384.0 * 64 * k, A.add, (a9,))
+    for d in range(4):
+        vh = fill(T.tab0[:, W * d + 2048:W * d + W], 0.0)
     need("v", fill(X("mk0"), 9e29))
     a1 = fill(X("mk0", 0, 2048, 4), -9e29)
     vmk = ts(X("mk"), X("mk0"), 4.0, A.mult, w=(a1,))
-    vh = None
-    for d in range(4):
-        vh = fill(T.tab0[:, W * d + 2048:W * d + W], 0.0)
 
     a1 = ts(X("t1"), X("nbt"), float(8192 * (3 - r)), A.add, w=(nbw,))
     vu = ts(X("ui"), X("nbt"), 8191, A.bitwise_and)
     vor = ts(X("orel"), X("t1"), 13, A.logical_shift_right, 3, A.bitwise_and, (a1,))
-    vuf = cp(X("uf"), X("ui"), (vu,))
     fl, ns = [], []
     for k in range(3):
         fl.append(ts(X("flg", 256 * k, 256 * k + 256), X("orel"), float(k), A.is_equal, w=(vor,)))
@@ -255,34 +277,45 @@ def rank_program(g, core, T, topo):
                                                  0.0, A.add, A.add)))
     vt = cp(X("tot", 0, 3), X("scn", 255, 768, 256), (ns[2],))
     pb = mm(X("msc", 0, 3), X("lt"), X("tot", 0, 3), (vt, glt))
+    a1 = ts(X("t2"), X("ui"), 2048.0, A.add, w=(vu,))
     vhf = ts(X("hf", 0, 3), X("tot", 0, 3), 0.5, A.mult, w=(vt,))
+    a2 = ts(X("uh"), X("t2"), 12, A.logical_shift_right, w=(a1,))
     vba = ts(X("ba", 0, 3), X("msc", 0, 3), -1.0, A.mult, 0.5, A.add, (pb,))
     vbs = tt(X("bas", 0, 3), X("msc", 0, 3), X("hf", 0, 3), A.subtract, (pb, vhf))
-    sab = []
-    need("s", vba, gsl)
-    for k in range(3):
-        sab.append(done("s", sc.activation(X("ab", 512 * k, 512 * k + 512), X("sl"), F.Abs, bias=col("ba", k))))
+    a3 = ts(X("ul"), X("t2"), 4095, A.bitwise_and)
+    vb64 = ts(X("b64", 0, 3), X("bas", 0, 3), 64.0, A.mult, w=(vbs,))
+    vuh = ts(X("uh16"), X("uh"), 16.0, A.mult, -64.0, A.add, (a2,))
+    vkl = ts(X("kl"), X("ul"), -2048.0, A.add, 1.0 / 256.0, A.mult, (a3,))
     kb = ["k0", "k1", "k2"]
-    sx, vg, jobs = [], [], []
+    sab, sgs, sx, vg, jobs = [], [], [], [], []
 
     tk = {}
     jobs.append(lambda: tk.update(a=ts(X("uq"), X("ui"), 11, A.logical_shift_right)))
     jobs.append(lambda: tk.update(fo=ts(X("fo"), X("orel"), 3.0, A.is_equal)))
-    jobs.append(lambda: tk.update(b=ts(X("c5"), X("uq"), 384.0, A.mult, -9727.0, A.add, (tk["a"],))))
-    jobs.append(lambda: tk.update(o=ts(X("c3"), X("orel"), 512.0, A.mult, -1.0, A.add)))
-    jobs.append(lambda: tk.update(c=tt(X("c6"), X("c5"), X("uf"), A.add, (tk["b"],))))
-    jobs.append(lambda: tk.update(d=tt(X("c1"), X("gm", 0, 256), X("gm", 256, 512), A.add, (vg[1],))))
-    jobs.append(lambda: tk.update(e=tt(X("c7"), X("c6"), X("fo"), A.mult, (tk["c"], tk["fo"]))))
-    jobs.append(lambda: tk.update(f=tt(X("c2"), X("c1"), X("gm", 512, 768), A.add, (tk["d"], vg[2]))))
-    jobs.append(lambda: tk.update(g=ts(X("c4"), X("c2"), 1.0 / 16384.0, A.mult, w=(tk["f"],))))
-    jobs.append(lambda: tk.update(h=tt(X("s2"), X("c4"), X("c3"), A.add, (tk["g"], tk["o"]))))
+    jobs.append(lambda: tk.update(u=cp(X("uf"), X("ui"))))
+    jobs.append(lambda: tk.update(d=tt(X("p2"), X("gm", 0, 256), X("gm", 256, 512), A.add, (vg[1],))))
+    jobs.append(lambda: tk.update(o=ts(X("p3"), X("orel"), 512.0, A.mult, -1.0, A.add)))
+    jobs.append(lambda: tk.update(f=tt(X("c2"), X("p2"), X("gm", 512, 768), A.add, (tk["d"], vg[2]))))
+    jobs.append(lambda: tk.update(b=ts(X("p0"), X("uq"), 384.0, A.mult, -9727.0, A.add, (tk["a"],))))
+    jobs.append(lambda: tk.update(g=ts(X("c4"), X("c2"), 1.0 / 64.0, A.mult, w=(tk["f"],))))
+    jobs.append(lambda: tk.update(c=tt(X("p0"), X("p0"), X("uf"), A.add, (tk["b"], tk["u"]))))
+    jobs.append(lambda: tk.update(h=tt(X("s2"), X("c4"), X("p3"), A.add, (tk["g"], tk["o"]))))
+    jobs.append(lambda: tk.update(e=tt(X("p1"), X("p0"), X("fo"), A.mult, (tk["c"], tk["fo"]))))
     jobs.append(lambda: tk.update(i=ts(X("a3"), X("s2"), 3, A.bitwise_and, w=(tk["h"],))))
     jobs.append(lambda: tk.update(j=ts(X("h2"), X("s2"), 2, A.logical_shift_right)))
-    jobs.append(lambda: tk.update(k=ts(X("c8"), X("a3"), float(W), A.mult, 2048.0, A.add, (tk["i"],))))
-    jobs.append(lambda: tk.update(l=tt(X("c9"), X("c8"), X("h2"), A.add, (tk["k"], tk["j"]))))
-    jobs.append(lambda: tk.update(z=tt(X("cde"), X("c9"), X("c7"), A.add, (tk["l"], tk["e"]))))
+    jobs.append(lambda: tk.update(k=ts(X("p2"), X("a3"), float(W), A.mult, 2048.0, A.add, (tk["i"],))))
+    jobs.append(lambda: tk.update(l=tt(X("c9"), X("p2"), X("h2"), A.add, (tk["k"], tk["j"]))))
+    jobs.append(lambda: tk.update(z=tt(X("cde"), X("c9"), X("p1"), A.add, (tk["l"], tk["e"]))))
+    jobs.pop(0)()
+    jobs.pop(0)()
 
     vr = []
+
+    def prepare(k):
+        need("s", vba, vb64, gsl)
+        sab.append(done("s", sc.activation(X("ab", 512 * k, 512 * k + 512), X("sl"), F.Abs, bias=col("ba", k))))
+        sgs.append(done("s", sc.activation(X("gs%d" % k), X("scn", 256 * k, 256 * k + 256), F.Identity, bias=col("b64", k),
+                                           scale=64.0)))
 
     def reduces(k):
         for m in range(4):
@@ -290,22 +323,25 @@ def rank_program(g, core, T, topo):
             need("v", sx[i])
             vr.append(done("v", v.tensor_reduce(col("rq0", i), X("xb", 256 * i, 256 * i + 256), AxisListType.X, A.min,
                                                 apply_absolute_value=True)))
-            if k * 4 + m < 5:
-                jobs.pop(0)()
 
+    prepare(0)
+    prepare(1)
     for k in range(3):
         c, e = 256 * k, 256 * k + 256
-        x1 = ts(X("gs", c, e), X("scn", c, e), col("bas", k), A.add, 16384.0, A.mult, (vbs,))
         voh = ts(X("oh", 512 * k, 512 * k + 512), X("ab", 512 * k, 512 * k + 512), col("hf", k), A.is_lt, w=(sab[k], vhf))
-        vg.append(tt(X("gm", c, e), X("gs", c, e), X("flg", c, e), A.mult, (x1,)))
-        vk = tt(X("key", c, e), X("gm", c, e), X("uf"), A.add, (vg[k], vuf))
+        vg.append(tt(X("gm", c, e), X("gs%d" % k), X("flg", c, e), A.mult, (sgs[k],)))
+        vk = tt(X("ka", c, e), X("gm", c, e), X("uh16"), A.add, (vg[k], vuh))
         for m in range(4):
             i = 4 * k + m
             ps = kb[i % 3]
-            p1 = mm(X(ps, 0, 256), X("oh", 512 * k + 128 * m, 512 * k + 128 * m + 128), X("key", c, e),
-                    (vk, voh) + ((sx[i - 3],) if i >= 3 else ()))
+            oh = X("oh", 512 * k + 128 * m, 512 * k + 128 * m + 128)
+            mm(X(ps, 0, 256), oh, X("kl"), (vkl, voh) + ((sx[i - 3],) if i >= 3 else ()), True, False)
+            p1 = mm(X(ps, 0, 256), oh, X("ka", c, e), (vk,), False, True)
             need("s", p1, vtb)
-            sx.append(done("s", sc.activation(X("xb", 256 * i, 256 * i + 256), X(ps, 0, 256), F.Identity, bias=col("tb", m))))
+            sx.append(done("s", sc.activation(X("xb", 256 * i, 256 * i + 256), X(ps, 0, 256), F.Identity, bias=col("tb", m),
+                                              scale=256.0)))
+        if k == 0:
+            prepare(2)
         if k:
             reduces(k - 1)
     reduces(2)
@@ -324,6 +360,11 @@ def rank_program(g, core, T, topo):
     mm(X("k0", 0, 256), X("e0"), X("cde"), (vcd, ge[1], sx[9]))
     pc = mm(X("k0", 256, 512), X("e1"), X("cde"))
 
+    pu = None
+    for k in range(3):
+        for h in range(2):
+            pu = mm(X("msc", 8 * k + 4 * h, 8 * k + 4 * h + 4), X(("e0", "e1")[h]), X("rq", 4 * k, 4 * k + 4),
+                    (("rqa", NIN), vbs, vba))
     if b == 0:
         xw = xl
     else:
@@ -333,26 +374,14 @@ def rank_program(g, core, T, topo):
     for m in range(4):
         po.append(mm(X("own", 512 * m, 512 * m + 512), X("idn"), T.tab0[:, 512 * m:512 * m + 512], (xown, gid)))
 
-    x1 = ts(X("w1"), X("k0"), col("qp"), A.is_lt, float(TW), A.mult, (pc,))
-    x2 = tt(X("w2"), X("w1"), X("k0"), A.add, (x1,))
-    voff = ts(X("offm"), X("w2"), col("qn"), A.add, w=(x2,))
-
-    pu = None
-    for k in range(3):
-        for h in range(2):
-            pu = mm(X("msc", 8 * k + 4 * h, 8 * k + 4 * h + 4), X(("e0", "e1")[h]), X("rq", 4 * k, 4 * k + 4),
-                    (("rqa", NIN), vbs, vba))
     x0 = cp(X("vi"), X("msc", 0, 24), (pu,))
+    xw1 = ts(X("vw"), X("msc", 0, 24), col("q2"), A.is_lt, float(TW), A.mult, (vq,))
     x1 = ts(X("vs"), X("vi"), 11, A.logical_shift_right, w=(x0,))
-    u4 = ts(X("v4"), X("vi"), 2, A.logical_shift_right)
-    x2 = ts(X("vc"), X("vs"), 384.0, A.mult, w=(x1,))
-    u3 = ts(X("v3"), X("vi"), 3, A.bitwise_and)
-    x3 = tt(X("vt"), X("vc"), X("vi"), A.add, (x2,))
-    o4 = cp(X("o4"), X("v4"), (u4,))
-    x4 = ts(X("vw"), X("vt"), col("qp"), A.is_lt, float(TW), A.mult, (x3,))
-    o3 = cp(X("o3"), X("v3"), (u3,))
-    x5 = tt(X("vz"), X("vt"), X("vw"), A.add, (x4,))
-    vou = ts(X("offu"), X("vz"), col("qn"), A.add, w=(x5,))
+    x2 = tt(X("vz"), X("vw"), X("msc", 0, 24), A.add, (xw1,))
+    x3 = ts(X("vc"), X("vs"), 384.0, A.mult, w=(x1,))
+    x4 = ts(X("vy"), X("vz"), col("qn"), A.add, w=(x2,))
+    x5 = tt(X("vt"), X("vc"), X("vy"), A.add, (x3, x4))
+    vou = cp(X("offu"), X("vt"), (x5,))
     need("v", xown, xw, vh, vou)
     vh0 = cp(T.h0[:], T.tab0[:, 0:TW].indirect(X("offu")))
     need("g", vh0)
@@ -361,12 +390,19 @@ def rank_program(g, core, T, topo):
         fused3([src[:, 128 * k:128 * k + 128] for k in range(3)],
                [dst[:, c0 + 128 * my[k]:c0 + 128 * my[k] + 128] for k in range(3)], sem)
     hsend(T.h0, T.lh0, 0, "ha0")
-    need("v", o4, cr)
-    y1 = cp(X("xg"), T.full[:, 0:2048].indirect(X("o4")))
+    u4 = ts(X("v4"), X("vi"), 2, A.logical_shift_right)
+    u3 = ts(X("v3"), X("vi"), 3, A.bitwise_and)
+    o4 = cp(X("o4"), X("v4"), (u4,))
+    o3 = cp(X("o3"), X("v3"), (u3,))
+    x1 = ts(X("w1"), X("k0"), col("qp"), A.is_lt, float(TW), A.mult, (pc,))
     need("v", o3, vm4)
     y2 = cp(X("mg"), X("m4").indirect(X("o3")))
+    need("v", o4, cr)
+    y1 = cp(X("xg"), T.full[:, 0:2048].indirect(X("o4")))
     y3 = tt(X("xm"), X("xg"), X("mg"), A.mult, (y1, y2))
     pz = mm(X("k1", 0, 384), X("bq"), X("xm"), (y3, gbq, sx[10]))
+    xk0 = tt(X("w2"), X("w1"), X("k0"), A.add, (x1,))
+    voff = ts(X("offm"), X("w2"), col("qn"), A.add, w=(xk0,))
     zt = [ts(X("z%d" % k), X("k1", k, 384, 4), col("m4", k), A.mult, w=(pz,)) for k in range(4)]
     y4 = tt(X("z4"), X("z0"), X("z1"), A.add, (zt[1],))
     y5 = tt(X("z5"), X("z2"), X("z3"), A.add, (zt[3],))
@@ -374,12 +410,22 @@ def rank_program(g, core, T, topo):
     y7 = ts(X("z7"), X("z6"), col("qp"), A.is_lt, float(TW), A.mult, (y6,))
     y8 = tt(X("z8"), X("z6"), X("z7"), A.add, (y7,))
     von = ts(X("offn"), X("z8"), col("qn"), A.add, w=(y8,))
-    need("y", ("ha0", NIN), vh0, xw)
-    dma("y", "ex", T.tab0[:, 2048:W], T.lh0[:])
-    ready = [rotate("y", "ex", T.tab0, 2048, 384, T.lh0), xw, xown]
+
+    bank = {1: xk0, 2: zt[3], 3: sx[11]}
+
+    def spread(src, s0, dst, c0, n, w, engs):
+        pt = [mm(X(kb[d - 1], 0, n), X("rot%d" % d), src[:, s0:s0 + n], tuple(w) + (gro[d - 1], bank[d])) for d in (1, 2, 3)]
+        for d, en in zip((1, 2, 3), engs):
+            bank[d] = (ac if en == "s" else cp)(dst[:, W * d + c0:W * d + c0 + n], X(kb[d - 1], 0, n), (pt[d - 1],))
+        return [bank[1], bank[2], bank[3]]
+
+    need("s", vh0)
+    need("v", vh0)
+    ready = spread(T.lh0, 0, T.tab0, 2048, 384, (("ha0", NIN),), "svs")
+    need("v", ("ha0", NIN))
+    ready += [cp(T.tab0[:, 2048:W], T.lh0[:]), xw, xown]
 
     hv = [None, T.h1, T.h2v]
-    lastv = von
     for s in range(3):
         tin = tabs[s]
         tout = tabs[s + 1] if s < 2 else T.res
@@ -388,7 +434,7 @@ def rank_program(g, core, T, topo):
             units.append((None, 0, 384, 0, "offn", 0))
         for c, (c0, n) in enumerate(CHUNKS):
             units.append((c, c0, n, 1536 + 4 * c0, "offm", c0 // 4))
-        need("s", von, voff, lastv, *ready)
+        need("s", von, voff, *ready)
         need("v", von, voff, vmk, *ready)
         sg, vgs = [], []
         for (c, c0, n, g0, of, k0) in units:
@@ -401,7 +447,8 @@ def rank_program(g, core, T, topo):
             vgs.append(cp(T.gat[:, g0 + e:g0 + 4 * n], tin[:, 0:TW].indirect(X(of, k0 + e // 16, k0 + n // 4))))
 
         vgather(0)
-        nready = []
+        ready = []
+        banked = 0
         for i, (c, c0, n, g0, of, k0) in enumerate(units):
             if i + 1 < len(units):
                 vgather(i + 1)
@@ -415,14 +462,19 @@ def rank_program(g, core, T, topo):
                 need("g", x2)
                 hsend(hv[s + 1], tout, 2048, "ha%d" % (s + 1))
                 continue
-            lastv = tt(tout[:, c0:c0 + n], T.sca[:, g0 + 3:g0 + 4 * n:4], T.own[:, c0:c0 + n], A.max, (x1, po[c0 // 512]))
+            lastv = tt(tout[:, c0:c0 + n], T.sca[:, g0 + 3:g0 + 4 * n:4], T.own[:, c0:c0 + n], A.max,
+                       (x1, po[c0 // 512], po[(c0 + n - 1) // 512]))
             if s < 2:
-                nready = [rotate("y", "ex", tout, c0, n, w=(lastv,))]
-                if c == 2:
-                    nready = [rotate("y", "ex", tout, 2048, 384, w=(("ha%d" % (s + 1), NIN),))]
-                if (c0 + n) % 512 == 0:
-                    m = c0 // 512
+                if c < 3:
+                    if c == 2:
+                        rotate("y", "ex", tout, 2048, 384, w=(("ha%d" % (s + 1), NIN),))
+                    exd = rotate("y", "ex", tout, c0, n, w=(lastv,))
+                else:
+                    ready += spread(tout, c0, tout, c0, n, (lastv,), "sss" if c == 3 else "vsv")
+                while banked < 4 and 512 * (banked + 1) <= c0 + n:
+                    m = banked
                     po[m] = mm(T.own[:, 512 * m:512 * m + 512], X("idn"), tout[:, 512 * m:512 * m + 512], (lastv,))
+                    banked += 1
             else:
                 for j, (o0, on, oc) in enumerate(OUTCH):
                     if oc != c:
@@ -436,9 +488,8 @@ def rank_program(g, core, T, topo):
                                      T.sem["oa%d_%d" % (b, j)], T.sem["ls"], pid, rid, m)
                         lsn[0] += bin(m).count("1")
                     else:
-                        lastj = j == len(OUTCH) - 1
                         for k in range(4):
-                            q = "s" if lastj and k % 2 else "y"
+                            q = "s" if j >= 2 and k % 2 else "y"
                             if k:
                                 m = topo.mask(team[r][k], core)
                                 need(q, ("oa%d_%d" % (k, j), bin(m).count("1")))
@@ -449,7 +500,7 @@ def rank_program(g, core, T, topo):
                                 yd = dma(q, "yd", T.y[32 * k:32 * k + 32, 2048 * h + o0:2048 * h + o0 + on],
                                          src[32 * h:32 * h + 32, o0:o0 + on])
         if s < 2:
-            ready = nready + [("ha%d" % (s + 1), NIN), lastv]
+            ready += [exd, ("ha%d" % (s + 1), NIN), lastv]
     if b == 0:
         need("y", yd)
     need("g", ("ls", lsn[0]))

from concourse.bass import DstId, RemoteDMATransfer
from concourse.mybir import AluOpType, AxisListType, ActivationFunctionType

N = 4
NCORES = 256
W = 2432
TW = 4 * W
CHUNKS = [(0, 512), (512, 512), (1024, 384), (1408, 384), (1792, 256)]
OUTCH = [(0, 1024, 1), (1024, 384, 2), (1408, 384, 3), (1792, 256, 4)]

SCRATCH = {}
WHERE = {}


def many(names, cols, dtype, where="sbuf", rows=128):
    for n in names.split():
        SCRATCH[n] = (where, [rows, cols], dtype)
        WHERE[n] = (n, 0, cols)


def pool(buf, names, cols, dtype):
    for i, n in enumerate(names.split()):
        WHERE[n] = (buf, i * cols, cols)
    SCRATCH[buf] = ("sbuf", [128, cols * len(names.split())], dtype)


many("nbt", 256, "int32")
pool("pi", "t1 orel ui s2 a3 h2 uq t2 uh ul", 256, "int32")
pool("pf", "uf c2 c4 c9 fo cde", 256, "float32")
many("flg scn", 768, "bfloat16")
many("zer", 256, "bfloat16")
many("tot", 4, "bfloat16")
pool("pmb", "lt idn oneb rot1 rot2 rot3", 128, "bfloat16")
pool("pm", "ones zf e0 e1 bq", 128, "float32")
many("sl w1 w2", 512, "float32")
many("ab", 1536, "float32")
many("oh", 1536, "float16")
many("ka", 768, "float16")
many("kl", 256, "float16")
pool("pc", "ba hf bas b64 tb m4 f1 f2 f3 s0 qp qn q2", 4, "float32")
many("gm", 768, "float32")
many("xb", 3072, "float32")
many("rq0 rqs rq", 12, "float32")
pool("pci", "ip iq i15 i16 i4", 1, "int32")
many("offm", 512, "uint16")
pool("pvi", "vi vs v4 v3", 24, "int32")
pool("pvf", "vc vt vw vz vy", 24, "float32")
pool("pvo", "offu o4 o3", 24, "uint16")
many("full", 2048, "float32")
many("cd", 2048, "float32", "dram", 16)
many("xg mg xm", 384, "float32")
pool("pz", "z0 z1 z2 z3 z4 z5 z6 z7 z8", 96, "float32")
many("offn", 96, "uint16")
many("tab0 tab1 tab2", TW, "bfloat16")
many("res mk0 mk st1 st2 st3 ot1 ot2 ot3", 2048, "bfloat16")
many("h0 h1 h2v lh0", 384, "bfloat16")
many("gat sca", 9728, "bfloat16")
many("own", 2048, "float32", "psum")
many("k0 k1 k2 msc", 512, "float32", "psum")
for _i, _n in enumerate("gs0 p0 gs1 p1 gs2 p2 uh16 p3".split()):
    WHERE[_n] = ("own", 256 * _i, 256)
SEMAPHORES = (["sv", "ss", "sp", "sg", "ex", "cw", "cr", "nbl", "xl0", "ld1", "ld2", "ld3", "nba", "xa", "rqa", "gi1", "gi2",
               "ha0", "ha1", "ha2", "ls", "yd"] + ["oa%d_%d" % (b, c) for b in (1, 2, 3) for c in range(len(OUTCH))])


def rank_program(g, core, T, topo):
    team = {}
    for r in range(N):
        rc = T.cores[r]
        team[r] = [rc] + [c for c in range(NCORES) if c != rc and topo.host(c) == topo.host(rc)
                          and topo.chip(c) == topo.chip(rc) and topo.die(c) == topo.die(rc)]
    r = b = None
    for rr in range(N):
        if core in team[rr]:
            r, b = rr, team[rr].index(core)
    if r is None:
        return
    A, F = AluOpType, ActivationFunctionType
    v, sc, pe, sy = g.vector, g.scalar, g.tensor, g.sync
    Q = {"v": v, "s": sc, "p": pe, "y": sy, "g": g}
    cnt, seen = {"v": 0, "s": 0, "p": 0, "g": 0}, {}

    def X(name, a=0, e=None, step=1, lo=0, hi=128):
        buf, c0, n = WHERE[name]
        e = n if e is None else e
        if step == 1:
            return T[buf][lo:hi, c0 + a:c0 + e]
        return T[buf][lo:hi, c0 + a:c0 + e:step]

    def col(name, k=0):
        return X(name, k, k + 1)

    def need(q, *tickets):
        for t in tickets:
            sem, n = t
            if seen.get((q, sem), 0) < n:
                Q[q].wait_ge(T.sem[sem], n)
                seen[(q, sem)] = n

    def done(q, ins):
        ins.then_inc(T.sem["s" + q], 1)
        cnt[q] += 1
        return ("s" + q, cnt[q])

    dcnt = {}

    def dma(q, sem, out, in_):
        Q[q].dma_start(out, in_).then_inc(T.sem[sem], 16)
        dcnt[sem] = dcnt.get(sem, 0) + 16
        return (sem, dcnt[sem])

    def ts(out, a, s1, op0, s2=None, op1=None, w=()):
        need("v", *w)
        if op1 is None:
            return done("v", v.tensor_scalar(out, a, s1, None, op0))
        return done("v", v.tensor_scalar(out, a, s1, s2, op0, op1))

    def tt(out, a, c, op, w=()):
        need("v", *w)
        return done("v", v.tensor_tensor(out, a, c, op))

    def cp(out, a, w=()):
        need("v", *w)
        return done("v", v.tensor_copy(out, a))

    def ac(out, a, w=()):
        need("s", *w)
        return done("s", sc.activation(out, a, F.Copy))

    def fill(ap, c):
        return done("v", v.memset(ap, c))

    def mm(out, l, rh, w=(), start=True, stop=True):
        need("p", *w)
        return done("p", pe.matmul(out, l, rh, start, stop))

    def bits(m):
        return [1 << i for i in range(16) if m >> i & 1]
    oth = [(r + 1 + k) % N for k in range(3)]
    peer = [team[o][b] for o in oth]
    my = [(r - o - 1) % N for o in oth]
    off = [p for p in peer if (topo.host(p), topo.chip(p)) != (topo.host(core), topo.chip(core))]
    offbits = bits(topo.mask(core, off[0]))
    half = len(offbits) // 2
    masks = []
    for p in peer:
        if p in off:
            k = off.index(p)
            masks.append(sum(offbits[k * half:(k + 1) * half]))
        else:
            masks.append(sum(x for x in bits(topo.mask(core, p)) if x not in offbits))
    NIN = sum(bin(m).count("1") for m in masks)
    lsn = [0]

    def did(p):
        rid, pid = topo.addr(p, core)
        return DstId(rid=rid, pnc=pid)

    def fused3(srcs, dsts, sem):
        tr = [RemoteDMATransfer(dst_ids=[did(p)], dma_engine_mask=masks[k], remote_sem=T.sem[sem],
                                srcs=[srcs[k]], dsts=[dsts[k]]) for k, p in enumerate(peer)]
        g.remote_dma_fused(tr, local_sem=T.sem["ls"])
        lsn[0] += NIN

    def rotate(q, sem, t, c0, n, w=()):
        need(q, *w)
        last = None
        for d in (1, 2, 3):
            cut = 128 - 32 * d
            last = dma(q, sem, t[0:cut, W * d + c0:W * d + c0 + n], t[32 * d:128, c0:c0 + n])
            last = dma(q, sem, t[cut:128, W * d + c0:W * d + c0 + n], t[0:32 * d, c0:c0 + n])
        return last

    tabs = [T.tab0, T.tab1, T.tab2]
    stage = [None, T.st1, T.st2, T.st3]

    xl = None
    if b == 0:
        def xload(k):
            for q in range(4):
                dma("ys"[q % 2], "ld%d" % k, stage[k][32 * q:32 * q + 32, :], T.x[32 * k:32 * k + 32, 2048 * q:2048 * q + 2048])
        for ch in range(8):
            nbw = dma("ys"[ch % 2], "nbl", T.nbt[16 * ch:16 * ch + 16, :], T.nb[:, 256 * ch:256 * ch + 256])
        xload(1)
        need("y", ("gi1", 1))
        need("s", ("gi1", 1))
        xload(2)
        xload(3)
        need("y", ("gi2", 1))
        for d in range(4):
            for q in range(4):
                s = 2048 * ((q + d) % 4)
                xl = dma("y", "xl0", T.tab0[32 * q:32 * q + 32, W * d:W * d + 2048], T.x[0:32, s:s + 2048])
    else:
        nbw = ("nba", 16)

    vob = fill(X("oneb"), 1.0)
    vo = fill(X("ones"), 1.0)
    vzf = fill(X("zf"), 0.0)
    vz = fill(X("zer"), 0.0)

    def sel(out, in_, pat, op, fl, base, cm, w=()):
        need("g", *w)
        return done("g", g.affine_select(out, in_, pat, op, fl, base, cm))

    def xsend(k):
        p = team[r][k]
        m = topo.mask(core, p)
        rid, pid = topo.addr(p, core)
        need("g", ("ld%d" % k, 64))
        g.remote_dma(T.tab0[:, 0:2048], stage[k][:], T.sem["xa"], T.sem["ls"], pid, rid, m)
        lsn[0] += bin(m).count("1")

    gip = done("g", g.iota(X("ip"), [[0, 1]], 0, 1))
    x1 = sel(X("lt"), X("oneb"), [[1, 128]], A.is_gt, 0.0, 0, -1, (vob,))
    glt = sel(X("lt"), X("lt"), [[1, 128]], A.not_equal, 0.5, 0, -1, (x1,))
    if b == 0:
        need("g", nbw)
        m = topo.mask(core, team[r][1])
        g.remote_dma_fused([RemoteDMATransfer(dst_ids=[did(p) for p in team[r][1:]], dma_engine_mask=m,
                                              remote_sem=T.sem["nba"], srcs=[T.nbt[:]], dsts=[T.nbt[:]] * 3)],
                           local_sem=T.sem["ls"])
        lsn[0] += bin(m).count("1")
        g.sem_inc(T.sem["gi1"], 1)
    gsl = None
    for k in range(4):
        gsl = done("g", g.iota(X("sl", 128 * k, 128 * k + 128), [[1, 4], [256, 2], [4, 16]], 64 * k, 0,
                               allow_small_or_imprecise_dtypes=True))
    ge = [sel(X(e), X("ones"), [[-32, 4], [0, 2], [-1, 16]], A.is_equal, 0.0, -16 * k, 1, (vo,))
          for k, e in enumerate(("e0", "e1"))]
    if b == 0:
        xsend(1)
    gid = sel(X("idn"), X("oneb"), [[1, 128]], A.is_equal, 0.0, 0, -1)
    gbq = None
    for k in range(4):
        gbq = sel(X("bq"), X("zf") if k == 0 else X("bq"), [[-16, 8], [0, 4], [-1, 4]], A.not_equal, 1.0, -4 * k, 1,
                  (vzf,) if k == 0 else (gbq,))
    if b == 0:
        xsend(2)
        xsend(3)
        g.sem_inc(T.sem["gi2"], 1)
    gro = [sel(X("rot%d" % d), X("zer", 0, 128), [[-1, 128]], A.not_equal, 1.0, -32 * d, 1, (vz,)) for d in (1, 2, 3)]
    gro = [sel(X("rot%d" % d), X("rot%d" % d), [[-1, 128]], A.not_equal, 1.0, 128 - 32 * d, 1, (gro[d - 1],)) for d in (1, 2, 3)]

    a1 = ts(X("iq"), X("ip"), 5, A.logical_shift_right, w=(gip,))
    a2 = ts(X("i15"), X("ip"), 15, A.bitwise_and)
    a3 = ts(X("i16"), X("ip"), 16, A.bitwise_and)
    a4 = ts(X("i4"), X("ip"), 2, A.logical_shift_right, 3, A.bitwise_and)
    a5 = ts(col("qp"), X("iq"), float(W), A.mult, w=(a1,))
    a5 = ts(col("qn"), X("iq"), float(-W), A.mult)
    vq = ts(col("q2"), X("iq"), 2048.0, A.mult)
    a6 = ts(col("f1"), X("i15"), 4.0, A.mult, w=(a2,))
    a7 = ts(col("f2"), X("i16"), 16.0, A.mult, w=(a3,))
    vm4 = None
    for k in range(4):
        vm4 = ts(col("m4", k), X("i4"), float(k), A.is_equal, w=(a4,))
    a8 = tt(col("f3"), col("f1"), col("f2"), A.add, (a6, a7))
    a9 = tt(col("s0"), col("f3"), X("iq"), A.add, (a8,))
    vtb = None
    for k in range(4):
        vtb = ts(col("tb", k), col("s0"), -16384.0, A.mult, -16384.0 * 64 * k, A.add, (a9,))
    for d in range(4):
        vh = fill(T.tab0[:, W * d + 2048:W * d + W], 0.0)
    need("v", fill(X("mk0"), 9e29))
    a1 = fill(X("mk0", 0, 2048, 4), -9e29)
    vmk = ts(X("mk"), X("mk0"), 4.0, A.mult, w=(a1,))

    a1 = ts(X("t1"), X("nbt"), float(8192 * (3 - r)), A.add, w=(nbw,))
    vu = ts(X("ui"), X("nbt"), 8191, A.bitwise_and)
    vor = ts(X("orel"), X("t1"), 13, A.logical_shift_right, 3, A.bitwise_and, (a1,))
    fl, ns = [], []
    for k in range(3):
        fl.append(ts(X("flg", 256 * k, 256 * k + 256), X("orel"), float(k), A.is_equal, w=(vor,)))
    for k in range(3):
        need("v", fl[k], vz)
        ns.append(done("v", v.tensor_tensor_scan(X("scn", 256 * k, 256 * k + 256), X("zer"), X("flg", 256 * k, 256 * k + 256),
                                                 0.0, A.add, A.add)))
    vt = cp(X("tot", 0, 3), X("scn", 255, 768, 256), (ns[2],))
    pb = mm(X("msc", 0, 3), X("lt"), X("tot", 0, 3), (vt, glt))
    a1 = ts(X("t2"), X("ui"), 2048.0, A.add, w=(vu,))
    vhf = ts(X("hf", 0, 3), X("tot", 0, 3), 0.5, A.mult, w=(vt,))
    a2 = ts(X("uh"), X("t2"), 12, A.logical_shift_right, w=(a1,))
    vba = ts(X("ba", 0, 3), X("msc", 0, 3), -1.0, A.mult, 0.5, A.add, (pb,))
    vbs = tt(X("bas", 0, 3), X("msc", 0, 3), X("hf", 0, 3), A.subtract, (pb, vhf))
    a3 = ts(X("ul"), X("t2"), 4095, A.bitwise_and)
    vb64 = ts(X("b64", 0, 3), X("bas", 0, 3), 64.0, A.mult, w=(vbs,))
    vuh = ts(X("uh16"), X("uh"), 16.0, A.mult, -64.0, A.add, (a2,))
    vkl = ts(X("kl"), X("ul"), -2048.0, A.add, 1.0 / 256.0, A.mult, (a3,))
    kb = ["k0", "k1", "k2"]
    sab, sgs, sx, vg, jobs = [], [], [], [], []

    tk = {}
    jobs.append(lambda: tk.update(a=ts(X("uq"), X("ui"), 11, A.logical_shift_right)))
    jobs.append(lambda: tk.update(fo=ts(X("fo"), X("orel"), 3.0, A.is_equal)))
    jobs.append(lambda: tk.update(u=cp(X("uf"), X("ui"))))
    jobs.append(lambda: tk.update(d=tt(X("p2"), X("gm", 0, 256), X("gm", 256, 512), A.add, (vg[1],))))
    jobs.append(lambda: tk.update(o=ts(X("p3"), X("orel"), 512.0, A.mult, -1.0, A.add)))
    jobs.append(lambda: tk.update(f=tt(X("c2"), X("p2"), X("gm", 512, 768), A.add, (tk["d"], vg[2]))))
    jobs.append(lambda: tk.update(b=ts(X("p0"), X("uq"), 384.0, A.mult, -9727.0, A.add, (tk["a"],))))
    jobs.append(lambda: tk.update(g=ts(X("c4"), X("c2"), 1.0 / 64.0, A.mult, w=(tk["f"],))))
    jobs.append(lambda: tk.update(c=tt(X("p0"), X("p0"), X("uf"), A.add, (tk["b"], tk["u"]))))
    jobs.append(lambda: tk.update(h=tt(X("s2"), X("c4"), X("p3"), A.add, (tk["g"], tk["o"]))))
    jobs.append(lambda: tk.update(e=tt(X("p1"), X("p0"), X("fo"), A.mult, (tk["c"], tk["fo"]))))
    jobs.append(lambda: tk.update(i=ts(X("a3"), X("s2"), 3, A.bitwise_and, w=(tk["h"],))))
    jobs.append(lambda: tk.update(j=ts(X("h2"), X("s2"), 2, A.logical_shift_right)))
    jobs.append(lambda: tk.update(k=ts(X("p2"), X("a3"), float(W), A.mult, 2048.0, A.add, (tk["i"],))))
    jobs.append(lambda: tk.update(l=tt(X("c9"), X("p2"), X("h2"), A.add, (tk["k"], tk["j"]))))
    jobs.append(lambda: tk.update(z=tt(X("cde"), X("c9"), X("p1"), A.add, (tk["l"], tk["e"]))))
    jobs.pop(0)()
    jobs.pop(0)()

    vr = []

    def prepare(k):
        need("s", vba, vb64, gsl)
        sab.append(done("s", sc.activation(X("ab", 512 * k, 512 * k + 512), X("sl"), F.Abs, bias=col("ba", k))))
        sgs.append(done("s", sc.activation(X("gs%d" % k), X("scn", 256 * k, 256 * k + 256), F.Identity, bias=col("b64", k),
                                           scale=64.0)))

    def reduces(k):
        for m in range(4):
            i = 4 * k + m
            need("v", sx[i])
            vr.append(done("v", v.tensor_reduce(col("rq0", i), X("xb", 256 * i, 256 * i + 256), AxisListType.X, A.min,
                                                apply_absolute_value=True)))

    prepare(0)
    prepare(1)
    for k in range(3):
        c, e = 256 * k, 256 * k + 256
        voh = ts(X("oh", 512 * k, 512 * k + 512), X("ab", 512 * k, 512 * k + 512), col("hf", k), A.is_lt, w=(sab[k], vhf))
        vg.append(tt(X("gm", c, e), X("gs%d" % k), X("flg", c, e), A.mult, (sgs[k],)))
        vk = tt(X("ka", c, e), X("gm", c, e), X("uh16"), A.add, (vg[k], vuh))
        for m in range(4):
            i = 4 * k + m
            ps = kb[i % 3]
            oh = X("oh", 512 * k + 128 * m, 512 * k + 128 * m + 128)
            mm(X(ps, 0, 256), oh, X("kl"), (vkl, voh) + ((sx[i - 3],) if i >= 3 else ()), True, False)
            p1 = mm(X(ps, 0, 256), oh, X("ka", c, e), (vk,), False, True)
            need("s", p1, vtb)
            sx.append(done("s", sc.activation(X("xb", 256 * i, 256 * i + 256), X(ps, 0, 256), F.Identity, bias=col("tb", m),
                                              scale=256.0)))
        if k == 0:
            prepare(2)
        if k:
            reduces(k - 1)
    reduces(2)
    vrq = ts(X("rqs"), X("rq0"), 8191.0, A.min, w=(vr[-1],))
    need("g", vrq)
    fused3([X("rqs", 4 * k, 4 * k + 4) for k in range(3)], [X("rq", 4 * my[k], 4 * my[k] + 4) for k in range(3)], "rqa")
    while jobs:
        jobs.pop(0)()
    vcd = tk["z"]
    need("s", vcd)
    for ch in range(8):
        cw = dma("s", "cw", T.cd[:, 256 * ch:256 * ch + 256], X("cde", lo=16 * ch, hi=16 * ch + 16))
    need("s", cw)
    for k in range(8):
        cr = dma("s", "cr", T.full[16 * k:16 * k + 16, :], T.cd[:, :])
    mm(X("k0", 0, 256), X("e0"), X("cde"), (vcd, ge[1], sx[9]))
    pc = mm(X("k0", 256, 512), X("e1"), X("cde"))

    pu = None
    for k in range(3):
        for h in range(2):
            pu = mm(X("msc", 8 * k + 4 * h, 8 * k + 4 * h + 4), X(("e0", "e1")[h]), X("rq", 4 * k, 4 * k + 4),
                    (("rqa", NIN), vbs, vba))
    if b == 0:
        xw = xl
    else:
        xw = rotate("y", "ex", T.tab0, 0, 2048, w=(("xa", 16),))
    xown = xl if b == 0 else ("xa", 16)
    po = []
    for m in range(4):
        po.append(mm(X("own", 512 * m, 512 * m + 512), X("idn"), T.tab0[:, 512 * m:512 * m + 512], (xown, gid)))

    x0 = cp(X("vi"), X("msc", 0, 24), (pu,))
    xw1 = ts(X("vw"), X("msc", 0, 24), col("q2"), A.is_lt, float(TW), A.mult, (vq,))
    x1 = ts(X("vs"), X("vi"), 11, A.logical_shift_right, w=(x0,))
    x2 = tt(X("vz"), X("vw"), X("msc", 0, 24), A.add, (xw1,))
    x3 = ts(X("vc"), X("vs"), 384.0, A.mult, w=(x1,))
    x4 = ts(X("vy"), X("vz"), col("qn"), A.add, w=(x2,))
    x5 = tt(X("vt"), X("vc"), X("vy"), A.add, (x3, x4))
    vou = cp(X("offu"), X("vt"), (x5,))
    need("v", xown, xw, vh, vou)
    vh0 = cp(T.h0[:], T.tab0[:, 0:TW].indirect(X("offu")))
    need("g", vh0)

    def hsend(src, dst, c0, sem):
        fused3([src[:, 128 * k:128 * k + 128] for k in range(3)],
               [dst[:, c0 + 128 * my[k]:c0 + 128 * my[k] + 128] for k in range(3)], sem)
    hsend(T.h0, T.lh0, 0, "ha0")
    u4 = ts(X("v4"), X("vi"), 2, A.logical_shift_right)
    u3 = ts(X("v3"), X("vi"), 3, A.bitwise_and)
    o4 = cp(X("o4"), X("v4"), (u4,))
    o3 = cp(X("o3"), X("v3"), (u3,))
    x1 = ts(X("w1"), X("k0"), col("qp"), A.is_lt, float(TW), A.mult, (pc,))
    need("v", o3, vm4)
    y2 = cp(X("mg"), X("m4").indirect(X("o3")))
    need("v", o4, cr)
    y1 = cp(X("xg"), T.full[:, 0:2048].indirect(X("o4")))
    y3 = tt(X("xm"), X("xg"), X("mg"), A.mult, (y1, y2))
    pz = mm(X("k1", 0, 384), X("bq"), X("xm"), (y3, gbq, sx[10]))
    xk0 = tt(X("w2"), X("w1"), X("k0"), A.add, (x1,))
    voff = ts(X("offm"), X("w2"), col("qn"), A.add, w=(xk0,))
    zt = [ts(X("z%d" % k), X("k1", k, 384, 4), col("m4", k), A.mult, w=(pz,)) for k in range(4)]
    y4 = tt(X("z4"), X("z0"), X("z1"), A.add, (zt[1],))
    y5 = tt(X("z5"), X("z2"), X("z3"), A.add, (zt[3],))
    y6 = tt(X("z6"), X("z4"), X("z5"), A.add, (y4, y5))
    y7 = ts(X("z7"), X("z6"), col("qp"), A.is_lt, float(TW), A.mult, (y6,))
    y8 = tt(X("z8"), X("z6"), X("z7"), A.add, (y7,))
    von = ts(X("offn"), X("z8"), col("qn"), A.add, w=(y8,))

    bank = {1: xk0, 2: zt[3], 3: sx[11]}

    def spread(src, s0, dst, c0, n, w, engs):
        pt = [mm(X(kb[d - 1], 0, n), X("rot%d" % d), src[:, s0:s0 + n], tuple(w) + (gro[d - 1], bank[d])) for d in (1, 2, 3)]
        for d, en in zip((1, 2, 3), engs):
            bank[d] = (ac if en == "s" else cp)(dst[:, W * d + c0:W * d + c0 + n], X(kb[d - 1], 0, n), (pt[d - 1],))
        return [bank[1], bank[2], bank[3]]

    need("s", vh0)
    need("v", vh0)
    ready = spread(T.lh0, 0, T.tab0, 2048, 384, (("ha0", NIN),), "svs")
    need("v", ("ha0", NIN))
    ready += [cp(T.tab0[:, 2048:W], T.lh0[:]), xw, xown]

    hv = [None, T.h1, T.h2v]
    for s in range(3):
        tin = tabs[s]
        tout = tabs[s + 1] if s < 2 else T.res
        units = []
        if s < 2:
            units.append((None, 0, 384, 0, "offn", 0))
        for c, (c0, n) in enumerate(CHUNKS):
            units.append((c, c0, n, 1536 + 4 * c0, "offm", c0 // 4))
        need("s", von, voff, *ready)
        need("v", von, voff, vmk, *ready)
        sg, vgs = [], []
        for (c, c0, n, g0, of, k0) in units:
            e = 3 * n
            sg.append(done("s", sc.activation(T.gat[:, g0:g0 + e], tin[:, 0:TW].indirect(X(of, k0, k0 + e // 16)), F.Copy)))

        def vgather(i):
            c, c0, n, g0, of, k0 = units[i]
            e = 3 * n
            vgs.append(cp(T.gat[:, g0 + e:g0 + 4 * n], tin[:, 0:TW].indirect(X(of, k0 + e // 16, k0 + n // 4))))

        vgather(0)
        ready = []
        banked = 0
        for i, (c, c0, n, g0, of, k0) in enumerate(units):
            if i + 1 < len(units):
                vgather(i + 1)
            need("v", sg[i], vgs[i])
            x1 = done("v", v.tensor_tensor_scan(T.sca[:, g0:g0 + 4 * n], T.mk[:, 0:4 * n], T.gat[:, g0:g0 + 4 * n], 0.0,
                                                A.min, A.max))
            if c is None:
                need("v", x1)
                x2 = done("v", v.tensor_tensor(hv[s + 1][:], tin[:, 0:TW].indirect(X("offu")),
                                               T.sca[:, g0 + 3:g0 + 4 * n:4], A.max))
                need("g", x2)
                hsend(hv[s + 1], tout, 2048, "ha%d" % (s + 1))
                continue
            lastv = tt(tout[:, c0:c0 + n], T.sca[:, g0 + 3:g0 + 4 * n:4], T.own[:, c0:c0 + n], A.max,
                       (x1, po[c0 // 512], po[(c0 + n - 1) // 512]))
            if s < 2:
                if c < 3:
                    if c == 2:
                        rotate("y", "ex", tout, 2048, 384, w=(("ha%d" % (s + 1), NIN),))
                    exd = rotate("y", "ex", tout, c0, n, w=(lastv,))
                else:
                    ready += spread(tout, c0, tout, c0, n, (lastv,), "sss" if c == 3 else "vsv")
                while banked < 4 and 512 * (banked + 1) <= c0 + n:
                    m = banked
                    po[m] = mm(T.own[:, 512 * m:512 * m + 512], X("idn"), tout[:, 512 * m:512 * m + 512], (lastv,))
                    banked += 1
            else:
                for j, (o0, on, oc) in enumerate(OUTCH):
                    if oc != c:
                        continue
                    if b:
                        p = team[r][0]
                        m = topo.mask(core, p)
                        rid, pid = topo.addr(p, core)
                        need("g", lastv)
                        g.remote_dma((None, T.ot1, T.ot2, T.ot3)[b][:, o0:o0 + on], T.res[:, o0:o0 + on],
                                     T.sem["oa%d_%d" % (b, j)], T.sem["ls"], pid, rid, m)
                        lsn[0] += bin(m).count("1")
                    else:
                        for k in range(4):
                            q = "s" if j >= 2 and k % 2 else "y"
                            if k:
                                m = topo.mask(team[r][k], core)
                                need(q, ("oa%d_%d" % (k, j), bin(m).count("1")))
                            else:
                                need(q, lastv)
                            src = (T.res, T.ot1, T.ot2, T.ot3)[k]
                            for h in range(4):
                                yd = dma(q, "yd", T.y[32 * k:32 * k + 32, 2048 * h + o0:2048 * h + o0 + on],
                                         src[32 * h:32 * h + 32, o0:o0 + on])
        if s < 2:
            ready += [exd, ("ha%d" % (s + 1), NIN), lastv]
    if b == 0:
        need("y", yd)
    need("g", ("ls", lsn[0]))
    for q in "vspg":
        need("y", ("s" + q, cnt[q]))
    if b == 0:
        need("y", xl)
    else:
        need("y", ("nba", 16), ("xa", 16))
    need("y", ("cr", dcnt["cr"]), ("cw", dcnt["cw"]), ("ex", dcnt["ex"]))
